import numpy as np
import ml_dtypes


def mxq(x, axis, fmt="e4m3"):
    dtype, down = {"e4m3": (ml_dtypes.float8_e4m3fn, 7), "e5m2": (ml_dtypes.float8_e5m2, 14)}[fmt]
    v = np.moveaxis(np.asarray(x, np.float32).astype(ml_dtypes.bfloat16).astype(np.float64), axis, -1)
    blocks = v.reshape(v.shape[:-1] + (-1, 32))
    amax = np.abs(blocks).max(-1, keepdims=True)
    byte = np.maximum(np.where(amax > 0, np.frexp(amax)[1] - 1 + 127, 0) - down, 1)
    scale = np.exp2(byte - 127.0)
    codes = (blocks / scale).astype(np.float32).astype(dtype).astype(np.float64)
    return np.moveaxis((codes * scale).reshape(v.shape), -1, axis)


WIDE = False


def mx_kscale(k):
    if not WIDE:
        return np.ones(k)
    levels = np.array([10, -10, 5, -5, 0])
    if k % 512:
        return np.exp2(np.random.permutation(np.resize(levels, k // 32))).repeat(32)
    a = np.empty((k // 512, 16))
    for p in range(k // 512):
        a[p, :8] = np.random.permutation(np.resize(levels, 8))
        for g in range(8):
            far = levels[np.abs(levels - a[p, g]) >= 10]
            a[p, g + 8] = far[np.random.randint(len(far))]
    return np.exp2(a.ravel()).repeat(32)


def f64(x):
    return np.asarray(x).astype(np.float64)


def striped(idx):
    return np.tile(idx.reshape(-1, 16).T, (8, 1)).astype(np.uint16)


def unstriped(offs):
    return offs[:16].T.reshape(-1).astype(np.int64)


E2M1 = np.array([0.0, 0.5, 1.0, 1.5, 2.0, 3.0, 4.0, 6.0, -0.0, -0.5, -1.0, -1.5, -2.0, -3.0, -4.0, -6.0])


def pack_weight(w, fmt):
    k, n = w.shape
    w = f64(np.asarray(w, np.float32).astype(ml_dtypes.bfloat16)).reshape(k // 32, 32, n)
    amax = np.abs(w).max(1)
    if fmt == "e4m3":
        byte = np.frexp(amax)[1] - 1 + 127 - 7
    else:
        mant, ex = np.frexp(amax / 6.0)
        byte = np.where(mant > 0.5, ex, ex - 1) + 127
    byte = np.clip(np.where(amax > 0, byte, 1), 1, 254)
    scaled = (w * np.exp2(127.0 - byte)[:, None, :]).reshape(k, n).astype(np.float32)
    by_word = np.ascontiguousarray(scaled.reshape(k // 512, 128, 4, n).transpose(0, 1, 3, 2))
    if fmt == "e4m3":
        words = by_word.astype(ml_dtypes.float8_e4m3fn).view(np.uint8)
    else:
        c = by_word.astype(ml_dtypes.float4_e2m1fn).view(np.uint8) & 0xF
        words = (c[..., 0::2] | (c[..., 1::2] << 4)).reshape(k // 512, 128, 2 * n)
    return np.ascontiguousarray(words), np.ascontiguousarray(byte.astype(np.uint8).reshape(k // 512, 16, n))


def unpack_weight(words, scales, fmt):
    g, _, n = scales.shape
    words = np.ascontiguousarray(words).reshape(g, 128, n, -1)
    if fmt == "e4m3":
        vals = words.view(ml_dtypes.float8_e4m3fn).astype(np.float64)
    else:
        nib = np.empty((g, 128, n, 4), np.uint8)
        nib[..., 0::2] = words & 0xF
        nib[..., 1::2] = words >> 4
        vals = E2M1[nib]
    vals = vals * np.repeat(np.exp2(scales.astype(np.float64) - 127.0), 8, axis=1)[..., None]
    return vals.transpose(0, 1, 3, 2).reshape(g * 512, n)


def gelu(v):
    return 0.5 * v * (1.0 + np.tanh(np.sqrt(2.0 / np.pi) * (v + 0.044715 * v**3)))


K, T, S, H, P = 512, 4096, 1024, 1024, 512

def setup_inputs():
    n = np.random.standard_normal
    s = mx_kscale(K)[:, None]
    u = mx_kscale(H)[:, None]
    tab_words, tab_scales = pack_weight(n((K, T)) * s, "e4m3")
    w2_words, w2_scales = pack_weight(n((K, H)) / np.sqrt(K) / s, "e2m1")
    w4_words, w4_scales = pack_weight(n((H, H)) / np.sqrt(H) / u, "e2m1")
    return {
        "tab_words": tab_words, "tab_scales": tab_scales,
        "offs": striped(np.random.permutation(T)[:S]),
        "pos1": striped(np.random.permutation(S)[:P]),
        "w1": (0.5 * n((K, H)) / np.sqrt(K) / s).astype(np.float32),
        "w2_words": w2_words, "w2_scales": w2_scales,
        "w3": (n((K, H)) / np.sqrt(K) / s).astype(np.float32),
        "speed": (1.6 * np.exp(0.4 * n((H, S)))).astype(np.float32),
        "gain": (0.8 * np.exp(0.3 * n(H)) * u[:, 0]).astype(np.float32),
        "w4_words": w4_words, "w4_scales": w4_scales,
        "w5": (n((H, H)) / np.sqrt(H) / u).astype(np.float32),
        "skip": (np.exp(0.3 * n(H)) / u[:, 0]).astype(np.float32),
        "wgo": np.exp(0.3 * n((128, P))).astype(np.float32),
    }

def reference(tab_words, tab_scales, offs, pos1, w1, w2_words, w2_scales, w3,
              speed, gain, w4_words, w4_scales, w5, skip, wgo):
    v = unpack_weight(tab_words, tab_scales, "e4m3")[:, unstriped(offs)]
    phase = mxq(f64(w1), 0, "e4m3").T @ v
    left = unpack_weight(w2_words, w2_scales, "e2m1").T @ v
    right = mxq(f64(w3), 0, "e4m3").T @ v
    h = f64(gain)[:, None] * (np.sin(phase) * f64(speed) + np.maximum(left, right))
    x = mxq(h[:, unstriped(pos1)], 0, "e4m3")
    y1 = unpack_weight(w4_words, w4_scales, "e2m1").T @ x
    y2 = mxq(f64(w5), 0, "e4m3").T @ x
    y = np.maximum(y1, y2)
    out = f64(skip)[:, None] * h
    out[:, unstriped(pos1)] = np.tile(f64(wgo), (H // 128, 1)) * y
    return out

@@ -1,0 +1,285 @@
+import math
+from contextlib import ExitStack
+
+import concourse.mybir as mybir
+
+K, T, S, H, NP = 512, 4096, 1024, 1024, 512
+FLOPS = 2 * (3 * K * H * S + 2 * H * H * NP)
+
+F32 = mybir.dt.float32
+BF16 = mybir.dt.bfloat16
+I32 = mybir.dt.int32
+U32 = mybir.dt.uint32
+U16 = mybir.dt.uint16
+U8 = mybir.dt.uint8
+FP8X4 = mybir.dt.float8_e4m3fn_x4
+FP4X4 = mybir.dt.float4_e2m1fn_x4
+ALU = mybir.AluOpType
+ACT = mybir.ActivationFunctionType
+
+P = 128
+PACK = 4
+PASS = P * PACK
+BANK = 512
+TILES = H // P
+TWO_PI = 2.0 * math.pi
+
+
+def tile_list_shellac_click_segments_kernel(
+    tc, tab_words, tab_scales, offs, pos1, w1, w2_words, w2_scales, w3, speed, gain, w4_words, w4_scales, w5, skip, wgo, out
+):
+    nc = tc.nc
+    with ExitStack() as ctx:
+        held = ctx.enter_context(tc.tile_pool(name="held", bufs=1))
+        ring = ctx.enter_context(tc.tile_pool(name="ring", bufs=2))
+        psum = ctx.enter_context(tc.psum_pool(name="psum", bufs=2))
+
+        idx = held.tile([P, S // 16], U16, name="idx")
+        p1 = held.tile([P, NP // 16], U16, name="p1")
+        tabw = held.tile([P, T], U32, name="tabw", align_bytes=64)
+        tabs = held.tile([P, T], U8, name="tabs", align_bytes=64)
+        w2w_raw = held.tile([P, H], U16, name="w2w_raw", align_bytes=64)
+        w2s_raw = held.tile([P, H], U8, name="w2s_raw", align_bytes=64)
+        w4w_raw = held.tile([P, 2, H], U16, name="w4w_raw", align_bytes=64)
+        w4s_raw = held.tile([P, 2, H], U8, name="w4s_raw", align_bytes=64)
+        w2w = held.tile([P, H], U16, name="w2w", align_bytes=64)
+        w2s = held.tile([P, H], U8, name="w2s", align_bytes=64)
+        w4w = held.tile([P, 2, H], U16, name="w4w", align_bytes=64)
+        w4s = held.tile([P, 2, H], U8, name="w4s", align_bytes=64)
+        gain_sb = held.tile([P, 2, PACK], F32, name="gain_sb")
+        skip_sb = held.tile([P, 2, PACK], F32, name="skip_sb")
+        wgo_sb = held.tile([P, PACK, NP], F32, name="wgo_sb")
+
+        nc.vector.memset(tabs[:].bitcast(I32), 0)
+        nc.vector.memset(w2s_raw[:].bitcast(I32), 0)
+        nc.vector.memset(w4s_raw[:].rearrange("p a c -> p (a c)").bitcast(I32), 0)
+
+        for q in range(4):
+            nc.sync.dma_start(out=tabs[32 * q : 32 * q + 4, :].bitcast(I32), in_=tab_scales[0, 4 * q : 4 * q + 4, :].bitcast(I32))
+        nc.sync.dma_start(idx[:], offs)
+        nc.sync.dma_start(out=w2w_raw[:].bitcast(I32), in_=w2_words[0].bitcast(I32))
+        nc.sync.dma_start(out=w4w_raw[:].bitcast(I32), in_=w4_words.rearrange("a p c -> p a c").bitcast(I32))
+        nc.sync.dma_start(out=tabw[:].bitcast(I32), in_=tab_words[0].rearrange("p t i -> p (t i)").bitcast(I32))
+
+        def load_weight(w, a, b):
+            raw = ring.tile([P, PACK, PASS], F32, name="raw", bufs=4)
+            nc.sync.dma_start(out=raw[:], in_=w[a * PASS : (a + 1) * PASS, b * PASS : (b + 1) * PASS].rearrange("(p j) c -> p j c", j=PACK))
+            return raw
+
+        def weave_weight(raw):
+            woven = ring.tile([P, PASS * PACK], BF16, name="woven", bufs=3, align_bytes=64)
+            nc.scalar.copy(
+                out=woven[:].rearrange("p (t m j) -> p m j t", t=PACK, j=PACK),
+                in_=raw[:].rearrange("p j (m t) -> p m j t", t=PACK),
+            )
+            return woven
+
+        def quantise(woven, label):
+            codes = held.tile([P, PASS], U32, name="codes_" + label, align_bytes=64)
+            scales = held.tile([P, PASS], U8, name="scales_" + label, align_bytes=64)
+            nc.vector.quantize_mx(out=codes[:].bitcast(FP8X4), scales=scales[:], in_=woven[:])
+            return codes, scales
+
+        def deal(dst, src):
+            nc.vector.tensor_copy(
+                out=dst.rearrange("p (b t m) -> p b t m", t=PACK, m=P),
+                in_=src.rearrange("p (b m t) -> p b t m", t=PACK, m=P),
+            )
+
+        def load_speed(i):
+            b, t = divmod(i, PACK)
+            sp = ring.tile([P, S], F32, name="row", bufs=7)
+            nc.sync.dma_start(out=sp[:], in_=speed[b * PASS : (b + 1) * PASS, :].rearrange("(p t) j -> p t j", t=PACK)[:, t, :])
+            return sp
+
+        raw1 = {0: load_weight(w1, 0, 0)}
+        for q in range(4):
+            nc.sync.dma_start(out=w2s_raw[32 * q : 32 * q + 4, :].bitcast(I32), in_=w2_scales[0, 4 * q : 4 * q + 4, :].bitcast(I32))
+        raw3 = {0: load_weight(w3, 0, 0)}
+        nc.sync.dma_start(out=gain_sb[:], in_=gain.rearrange("(b p t) -> p b t", p=P, t=PACK))
+        nc.sync.dma_start(p1[:], pos1)
+        speeds = {i: load_speed(i) for i in range(2)}
+        raw1[1] = load_weight(w1, 0, 1)
+        raw3[1] = load_weight(w3, 0, 1)
+        for q in range(4):
+            nc.sync.dma_start(
+                out=w4s_raw[32 * q : 32 * q + 4, :, :].bitcast(I32),
+                in_=w4_scales[:, 4 * q : 4 * q + 4, :].rearrange("a r c -> r a c").bitcast(I32),
+            )
+        for i in range(2, 7):
+            speeds[i] = load_speed(i)
+
+        deal(w2w[:], w2w_raw[:])
+        deal(w4w[:].rearrange("p a c -> p (a c)"), w4w_raw[:].rearrange("p a c -> p (a c)"))
+
+        vw, vs = [], []
+        for half in range(2):
+            words = held.tile([P, BANK], U32, name="vw%d" % half, align_bytes=64)
+            sbytes = held.tile([P, BANK], U8, name="vs%d" % half, align_bytes=64)
+            cols = idx[:, half * (BANK // 16) : (half + 1) * (BANK // 16)]
+            nc.vector.tensor_copy(words[:], tabw[:].indirect(cols))
+            nc.vector.tensor_copy(sbytes[:], tabs[:].indirect(cols))
+            vw.append(words)
+            vs.append(sbytes)
+        deal(w2s[:], w2s_raw[:])
+
+        q1 = {0: quantise(weave_weight(raw1[0]), "w1_0")}
+        q3 = {0: quantise(weave_weight(raw3[0]), "w3_0")}
+        q5, raw5, woven5 = {}, {}, {}
+        xq, picked = {}, {}
+        hs, state = {}, {}
+
+        def mx(acc, lw, ls, rw, rs, start, stop):
+            nc.tensor.matmul_mx(out=acc, lhsT=lw, lhsT_scale=ls, rhs=rw, rhs_scale=rs, start=start, stop=stop)
+
+        def products(i):
+            b, t = divmod(i, PACK)
+            cols = slice(t * P, (t + 1) * P)
+            wide = slice(i * P, (i + 1) * P)
+            ph, lf, rt = [], [], []
+            for half in range(2):
+                acc = psum.tile([P, BANK], F32, name="phase", bufs=4)
+                mx(acc[:], q1[b][0][:, cols].bitcast(FP8X4), q1[b][1][:, cols], vw[half][:].bitcast(FP8X4), vs[half][:], True, True)
+                ph.append(acc)
+            for half in range(2):
+                acc = psum.tile([P, BANK], F32, name="left")
+                mx(acc[:], w2w[:, wide].bitcast(FP4X4), w2s[:, wide], vw[half][:].bitcast(FP8X4), vs[half][:], True, True)
+                lf.append(acc)
+            for half in range(2):
+                acc = psum.tile([P, BANK], F32, name="right")
+                mx(acc[:], q3[b][0][:, cols].bitcast(FP8X4), q3[b][1][:, cols], vw[half][:].bitcast(FP8X4), vs[half][:], True, True)
+                rt.append(acc)
+            state[i] = {"ph": ph, "lf": lf, "rt": rt}
+
+        def halfcols(half):
+            return slice(half * BANK, (half + 1) * BANK)
+
+        def turns(i):
+            st = state[i]
+            st["k"] = ring.tile([P, S], I32, name="turns")
+            st["m"] = ring.tile([P, S], F32, name="larger", bufs=3)
+            for half in range(2):
+                nc.scalar.copy(out=st["m"][:, halfcols(half)], in_=st["lf"][half][:])
+            for half in range(2):
+                nc.vector.tensor_scalar(st["k"][:, halfcols(half)], st["ph"][half][:], 1.0 / TWO_PI, 0.5, ALU.mult, ALU.add)
+
+        def fraction(i):
+            st = state[i]
+            st["f"] = ring.tile([P, S], F32, name="frac", bufs=3)
+            for half in range(2):
+                nc.vector.scalar_tensor_tensor(
+                    st["f"][:, halfcols(half)], st["ph"][half][:], 1.0 / TWO_PI, st["k"][:, halfcols(half)], ALU.mult, ALU.subtract
+                )
+            nc.scalar.activation(st["f"][:], st["f"][:], ACT.Sin, bias=-math.pi, scale=-TWO_PI)
+
+        def larger(i):
+            st = state[i]
+            for half in range(2):
+                nc.vector.tensor_tensor(st["m"][:, halfcols(half)], st["rt"][half][:], st["m"][:, halfcols(half)], ALU.max)
+
+        def wobble(i):
+            b, t = divmod(i, PACK)
+            st = state[i]
+            nc.vector.scalar_tensor_tensor(st["f"][:], st["f"][:], gain_sb[:, b, t : t + 1], speeds[i][:], ALU.mult, ALU.mult)
+
+        def feature(i):
+            b, t = divmod(i, PACK)
+            st = state[i]
+            hs[i] = held.tile([P, S], F32, name="h%d" % i)
+            nc.vector.scalar_tensor_tensor(hs[i][:], st["m"][:], gain_sb[:, b, t : t + 1], st["f"][:], ALU.mult, ALU.add)
+
+        def pick(i):
+            b, t = divmod(i, PACK)
+            if t == 0:
+                picked[b] = ring.tile([P, PACK, NP], BF16, name="picked")
+            nc.vector.tensor_copy(picked[b][:, t, :], hs[i][:].indirect(p1[:]))
+
+        def weave_picked(b, engine_copy):
+            woven = ring.tile([P, NP * PACK], BF16, name="woven", bufs=3, align_bytes=64)
+            engine_copy(
+                out=woven[:].rearrange("p (c i t) -> p c t i", i=4, t=PACK),
+                in_=picked[b][:].rearrange("p t (c i) -> p c t i", i=4),
+            )
+            return woven
+
+        extra = {}
+        products(0)
+        for i in range(TILES + 1):
+            if i < TILES:
+                turns(i)
+            if i > 0:
+                wobble(i - 1)
+            if i == 1:
+                speeds[7] = load_speed(7)
+                for a, b in ((0, 0), (1, 0), (0, 1), (1, 1)):
+                    raw5[a, b] = load_weight(w5, a, b)
+                nc.sync.dma_start(out=skip_sb[:], in_=skip.rearrange("(b p t) -> p b t", p=P, t=PACK))
+                for q in range(4):
+                    nc.sync.dma_start(out=wgo_sb[32 * q : 32 * (q + 1), :, :], in_=wgo.rearrange("(p t) m -> p t m", t=PACK))
+            if i < TILES:
+                fraction(i)
+            if i > 0:
+                feature(i - 1)
+            if i < TILES:
+                larger(i)
+            if i == 0:
+                extra["w1"] = weave_weight(raw1[1])
+            if i == 1:
+                extra["w3"] = weave_weight(raw3[1])
+                q1[1] = quantise(extra["w1"], "w1_1")
+            if i == 2:
+                q3[1] = quantise(extra["w3"], "w3_1")
+                woven5[0, 0] = weave_weight(raw5[0, 0])
+            if i == 3:
+                q5[0, 0] = quantise(woven5[0, 0], "w5_00")
+                woven5[1, 0] = weave_weight(raw5[1, 0])
+            if i == 4:
+                q5[1, 0] = quantise(woven5[1, 0], "w5_10")
+                deal(w4s[:].rearrange("p a c -> p (a c)"), w4s_raw[:].rearrange("p a c -> p (a c)"))
+            if i == 5:
+                extra["x0"] = weave_picked(0, nc.scalar.copy)
+            if i == 6:
+                xq[0] = quantise(extra["x0"], "x0")
+                woven5[0, 1] = weave_weight(raw5[0, 1])
+            if i == 7:
+                woven5[1, 1] = weave_weight(raw5[1, 1])
+            if i + 1 < TILES:
+                products(i + 1)
+            if i > 0:
+                pick(i - 1)
+
+        extra["x1"] = weave_picked(1, nc.vector.tensor_copy)
+        q5[0, 1] = quantise(woven5[0, 1], "w5_01")
+        xq[1] = quantise(extra["x1"], "x1")
+        q5[1, 1] = quantise(woven5[1, 1], "w5_11")
+
+        second = {}
+
+        def second_products(i):
+            b, t = divmod(i, PACK)
+            cols = slice(t * P, (t + 1) * P)
+            wide = slice(i * P, (i + 1) * P)
+            y1 = psum.tile([P, NP], F32, name="phase", bufs=4)
+            for a in range(2):
+                mx(y1[:], w4w[:, a, wide].bitcast(FP4X4), w4s[:, a, wide], xq[a][0][:].bitcast(FP8X4), xq[a][1][:], a == 0, a == 1)
+            y2 = psum.tile([P, NP], F32, name="right")
+            for a in range(2):
+                mx(y2[:], q5[a, b][0][:, cols].bitcast(FP8X4), q5[a, b][1][:, cols], xq[a][0][:].bitcast(FP8X4), xq[a][1][:], a == 0, a == 1)
+            y = ring.tile([P, NP], F32, name="y", bufs=3)
+            nc.scalar.copy(out=y[:], in_=y1[:])
+            page = ring.tile([P, S], F32, name="row", bufs=7)
+            nc.scalar.activation(page[:], hs[i][:], ACT.Copy, scale=skip_sb[:, b, t : t + 1])
+            nc.vector.tensor_tensor(y[:], y2[:], y[:], ALU.max)
+            second[i] = (y, page)
+
+        def put(i):
+            b, t = divmod(i, PACK)
+            y, page = second[i]
+            nc.vector.tensor_tensor(page[:].indirect(p1[:]), y[:], wgo_sb[:, t, :], ALU.mult)
+            nc.sync.dma_start(out=out[b * PASS : (b + 1) * PASS, :].rearrange("(p t) j -> p t j", t=PACK)[:, t, :], in_=page[:])
+
+        second_products(0)
+        for i in range(TILES):
+            if i + 1 < TILES:
+                second_products(i + 1)
+            put(i)

@@ -2,6 +2,7 @@ import math
 from contextlib import ExitStack
 
 import concourse.mybir as mybir
+from concourse.masks import make_identity
 
 K, T, S, H, NP = 512, 4096, 1024, 1024, 512
 FLOPS = 2 * (3 * K * H * S + 2 * H * H * NP)
@@ -22,6 +23,8 @@ PACK = 4
 PASS = P * PACK
 BANK = 512
 TILES = H // P
+CHUNK = 256
+HALF = NP // 2
 TWO_PI = 2.0 * math.pi
 
 
@@ -38,139 +41,130 @@ def tile_list_shellac_click_segments_kernel(
         p1 = held.tile([P, NP // 16], U16, name="p1")
         tabw = held.tile([P, T], U32, name="tabw", align_bytes=64)
         tabs = held.tile([P, T], U8, name="tabs", align_bytes=64)
-        w2w_raw = held.tile([P, H], U16, name="w2w_raw", align_bytes=64)
-        w2s_raw = held.tile([P, H], U8, name="w2s_raw", align_bytes=64)
-        w4w_raw = held.tile([P, 2, H], U16, name="w4w_raw", align_bytes=64)
-        w4s_raw = held.tile([P, 2, H], U8, name="w4s_raw", align_bytes=64)
         w2w = held.tile([P, H], U16, name="w2w", align_bytes=64)
         w2s = held.tile([P, H], U8, name="w2s", align_bytes=64)
         w4w = held.tile([P, 2, H], U16, name="w4w", align_bytes=64)
         w4s = held.tile([P, 2, H], U8, name="w4s", align_bytes=64)
-        gain_sb = held.tile([P, 2, PACK], F32, name="gain_sb")
-        skip_sb = held.tile([P, 2, PACK], F32, name="skip_sb")
-        wgo_sb = held.tile([P, PACK, NP], F32, name="wgo_sb")
+        wgo_sb = held.tile([P, NP], F32, name="wgo_sb")
+        rows = held.tile([P, P], F32, name="rows")
+        factors = held.tile([P, 3 * TILES], F32, name="factors")
+        ident = held.tile([P, P], F32, name="ident")
+        ident16 = held.tile([P, P], BF16, name="ident16")
 
         nc.vector.memset(tabs[:].bitcast(I32), 0)
-        nc.vector.memset(w2s_raw[:].bitcast(I32), 0)
-        nc.vector.memset(w4s_raw[:].rearrange("p a c -> p (a c)").bitcast(I32), 0)
+        nc.vector.memset(w2s[:].bitcast(I32), 0)
+        nc.vector.memset(w4s[:].rearrange("p a c -> p (a c)").bitcast(I32), 0)
+        nc.gpsimd.memset(rows[:], 0.0)
+        make_identity(nc, ident[:])
+        make_identity(nc, ident16[:])
+
+        def load_weight(w, a, c0, width, name, bufs):
+            raw = ring.tile([P, PACK, width], F32, name=name, bufs=bufs)
+            nc.sync.dma_start(out=raw[:], in_=w[a * PASS : (a + 1) * PASS, c0 : c0 + width].rearrange("(p j) c -> p j c", j=PACK))
+            return raw
+
+        def load_first(w, c):
+            return load_weight(w, 0, c * CHUNK, CHUNK, "raw", 4)
+
+        def weave(woven, raw, c0, c1):
+            nc.scalar.copy(
+                out=woven[:].rearrange("p (c i j) -> p c j i", i=4, j=PACK)[:, c0 // 4 : c1 // 4],
+                in_=raw[:].rearrange("p j (c i) -> p c j i", i=4)[:, c0 // 4 : c1 // 4],
+            )
+
+        def weave_first(raw):
+            woven = ring.tile([P, CHUNK * PACK], BF16, name="woven", bufs=3, align_bytes=64)
+            weave(woven, raw, 0, CHUNK)
+            return woven
+
+        def quantise(woven, width, label, slot=None):
+            codes = held.tile([P, width], U32, name=slot or "codes_" + label, align_bytes=64)
+            scales = held.tile([P, width], U8, name="scales_" + label, align_bytes=64)
+            nc.vector.quantize_mx(out=codes[:].bitcast(FP8X4), scales=scales[:], in_=woven[:])
+            return codes, scales
+
+        def load_speed(i):
+            sp = ring.tile([P, S], F32, name="speed", bufs=4)
+            nc.sync.dma_start(out=sp[:], in_=speed[i * P : (i + 1) * P, :])
+            return sp
 
         for q in range(4):
             nc.sync.dma_start(out=tabs[32 * q : 32 * q + 4, :].bitcast(I32), in_=tab_scales[0, 4 * q : 4 * q + 4, :].bitcast(I32))
         nc.sync.dma_start(idx[:], offs)
-        nc.sync.dma_start(out=w2w_raw[:].bitcast(I32), in_=w2_words[0].bitcast(I32))
-        nc.sync.dma_start(out=w4w_raw[:].bitcast(I32), in_=w4_words.rearrange("a p c -> p a c").bitcast(I32))
-        nc.sync.dma_start(out=tabw[:].bitcast(I32), in_=tab_words[0].rearrange("p t i -> p (t i)").bitcast(I32))
-
-        def load_weight(w, a, b):
-            raw = ring.tile([P, PACK, PASS], F32, name="raw", bufs=4)
-            nc.sync.dma_start(out=raw[:], in_=w[a * PASS : (a + 1) * PASS, b * PASS : (b + 1) * PASS].rearrange("(p j) c -> p j c", j=PACK))
-            return raw
-
-        def weave_weight(raw):
-            woven = ring.tile([P, PASS * PACK], BF16, name="woven", bufs=3, align_bytes=64)
-            nc.scalar.copy(
-                out=woven[:].rearrange("p (t m j) -> p m j t", t=PACK, j=PACK),
-                in_=raw[:].rearrange("p j (m t) -> p m j t", t=PACK),
-            )
-            return woven
-
-        def quantise(woven, label):
-            codes = held.tile([P, PASS], U32, name="codes_" + label, align_bytes=64)
-            scales = held.tile([P, PASS], U8, name="scales_" + label, align_bytes=64)
-            nc.vector.quantize_mx(out=codes[:].bitcast(FP8X4), scales=scales[:], in_=woven[:])
-            return codes, scales
-
-        def deal(dst, src):
-            nc.vector.tensor_copy(
-                out=dst.rearrange("p (b t m) -> p b t m", t=PACK, m=P),
-                in_=src.rearrange("p (b m t) -> p b t m", t=PACK, m=P),
-            )
-
-        def load_speed(i):
-            b, t = divmod(i, PACK)
-            sp = ring.tile([P, S], F32, name="row", bufs=7)
-            nc.sync.dma_start(out=sp[:], in_=speed[b * PASS : (b + 1) * PASS, :].rearrange("(p t) j -> p t j", t=PACK)[:, t, :])
-            return sp
-
-        raw1 = {0: load_weight(w1, 0, 0)}
-        for q in range(4):
-            nc.sync.dma_start(out=w2s_raw[32 * q : 32 * q + 4, :].bitcast(I32), in_=w2_scales[0, 4 * q : 4 * q + 4, :].bitcast(I32))
-        raw3 = {0: load_weight(w3, 0, 0)}
-        nc.sync.dma_start(out=gain_sb[:], in_=gain.rearrange("(b p t) -> p b t", p=P, t=PACK))
         nc.sync.dma_start(p1[:], pos1)
-        speeds = {i: load_speed(i) for i in range(2)}
-        raw1[1] = load_weight(w1, 0, 1)
-        raw3[1] = load_weight(w3, 0, 1)
+        nc.sync.dma_start(out=rows[0:TILES, :], in_=gain.rearrange("(i p) -> i p", p=P))
+        raw1 = {0: load_first(w1, 0)}
+        nc.sync.dma_start(out=w2w[:].bitcast(I32), in_=w2_words[0].bitcast(I32))
+        nc.sync.dma_start(out=tabw[:].bitcast(I32), in_=tab_words[0].rearrange("p t i -> p (t i)").bitcast(I32))
         for q in range(4):
-            nc.sync.dma_start(
-                out=w4s_raw[32 * q : 32 * q + 4, :, :].bitcast(I32),
-                in_=w4_scales[:, 4 * q : 4 * q + 4, :].rearrange("a r c -> r a c").bitcast(I32),
-            )
-        for i in range(2, 7):
-            speeds[i] = load_speed(i)
-
-        deal(w2w[:], w2w_raw[:])
-        deal(w4w[:].rearrange("p a c -> p (a c)"), w4w_raw[:].rearrange("p a c -> p (a c)"))
+            nc.sync.dma_start(out=w2s[32 * q : 32 * q + 4, :].bitcast(I32), in_=w2_scales[0, 4 * q : 4 * q + 4, :].bitcast(I32))
+        raw3 = {0: load_first(w3, 0)}
+        speeds = {0: load_speed(0)}
+        nc.sync.dma_start(out=rows[TILES : 2 * TILES, :], in_=skip.rearrange("(i p) -> i p", p=P))
+        for c in range(1, 4):
+            raw1[c] = load_first(w1, c)
+            raw3[c] = load_first(w3, c)
+            speeds[c] = load_speed(c)
 
         vw, vs = [], []
         for half in range(2):
-            words = held.tile([P, BANK], U32, name="vw%d" % half, align_bytes=64)
             sbytes = held.tile([P, BANK], U8, name="vs%d" % half, align_bytes=64)
-            cols = idx[:, half * (BANK // 16) : (half + 1) * (BANK // 16)]
-            nc.vector.tensor_copy(words[:], tabw[:].indirect(cols))
-            nc.vector.tensor_copy(sbytes[:], tabs[:].indirect(cols))
-            vw.append(words)
+            nc.vector.tensor_copy(sbytes[:], tabs[:].indirect(idx[:, half * (BANK // 16) : (half + 1) * (BANK // 16)]))
             vs.append(sbytes)
-        deal(w2s[:], w2s_raw[:])
+        q1 = {0: quantise(weave_first(raw1[0]), CHUNK, "w1_0")}
+        for half in range(2):
+            words = held.tile([P, BANK], U32, name="vw%d" % half, align_bytes=64)
+            nc.vector.tensor_copy(words[:], tabw[:].indirect(idx[:, half * (BANK // 16) : (half + 1) * (BANK // 16)]))
+            vw.append(words)
+        q3 = {0: quantise(weave_first(raw3[0]), CHUNK, "w3_0")}
 
-        q1 = {0: quantise(weave_weight(raw1[0]), "w1_0")}
-        q3 = {0: quantise(weave_weight(raw3[0]), "w3_0")}
-        q5, raw5, woven5 = {}, {}, {}
-        xq, picked = {}, {}
-        hs, state = {}, {}
+        q5, raw5, woven, xq, turned, state, us = {}, {}, {}, {}, {}, {}, {}
 
         def mx(acc, lw, ls, rw, rs, start, stop):
             nc.tensor.matmul_mx(out=acc, lhsT=lw, lhsT_scale=ls, rhs=rw, rhs_scale=rs, start=start, stop=stop)
 
-        def products(i):
-            b, t = divmod(i, PACK)
-            cols = slice(t * P, (t + 1) * P)
-            wide = slice(i * P, (i + 1) * P)
-            ph, lf, rt = [], [], []
-            for half in range(2):
-                acc = psum.tile([P, BANK], F32, name="phase", bufs=4)
-                mx(acc[:], q1[b][0][:, cols].bitcast(FP8X4), q1[b][1][:, cols], vw[half][:].bitcast(FP8X4), vs[half][:], True, True)
-                ph.append(acc)
-            for half in range(2):
-                acc = psum.tile([P, BANK], F32, name="left")
-                mx(acc[:], w2w[:, wide].bitcast(FP4X4), w2s[:, wide], vw[half][:].bitcast(FP8X4), vs[half][:], True, True)
-                lf.append(acc)
-            for half in range(2):
-                acc = psum.tile([P, BANK], F32, name="right")
-                mx(acc[:], q3[b][0][:, cols].bitcast(FP8X4), q3[b][1][:, cols], vw[half][:].bitcast(FP8X4), vs[half][:], True, True)
-                rt.append(acc)
-            state[i] = {"ph": ph, "lf": lf, "rt": rt}
-
         def halfcols(half):
             return slice(half * BANK, (half + 1) * BANK)
 
-        def turns(i):
-            st = state[i]
-            st["k"] = ring.tile([P, S], I32, name="turns")
-            st["m"] = ring.tile([P, S], F32, name="larger", bufs=3)
+        def phase_products(i):
+            c, cols = i // 2, slice((i % 2) * P, (i % 2 + 1) * P)
+            state[i] = {"ph": []}
             for half in range(2):
-                nc.scalar.copy(out=st["m"][:, halfcols(half)], in_=st["lf"][half][:])
-            for half in range(2):
-                nc.vector.tensor_scalar(st["k"][:, halfcols(half)], st["ph"][half][:], 1.0 / TWO_PI, 0.5, ALU.mult, ALU.add)
+                acc = psum.tile([P, BANK], F32, name="phase")
+                mx(acc[:], q1[c][0][:, cols].bitcast(FP8X4), q1[c][1][:, cols], vw[half][:].bitcast(FP8X4), vs[half][:], True, True)
+                state[i]["ph"].append(acc)
 
-        def fraction(i):
+        def pair_products(i):
+            c, cols, wide = i // 2, slice((i % 2) * P, (i % 2 + 1) * P), slice(i * P, (i + 1) * P)
             st = state[i]
-            st["f"] = ring.tile([P, S], F32, name="frac", bufs=3)
+            st["rt"] = []
+            if i == TILES - 1:
+                st["m"] = held.tile([P, S], F32, name="last_larger", align_bytes=64)
+            else:
+                st["m"] = ring.tile([P, S], F32, name="larger", bufs=3)
+            for half in range(2):
+                lf = psum.tile([P, BANK], F32, name="left")
+                mx(lf[:], w2w[:, wide].bitcast(FP4X4), w2s[:, wide], vw[half][:].bitcast(FP8X4), vs[half][:], True, True)
+                nc.scalar.copy(out=st["m"][:, halfcols(half)], in_=lf[:])
+            for half in range(2):
+                acc = psum.tile([P, BANK], F32, name="right")
+                mx(acc[:], q3[c][0][:, cols].bitcast(FP8X4), q3[c][1][:, cols], vw[half][:].bitcast(FP8X4), vs[half][:], True, True)
+                st["rt"].append(acc)
+
+        def sine(i):
+            st = state[i]
+            turns = ring.tile([P, S], I32, name="turns", bufs=1)
+            if i == TILES - 1:
+                st["f"] = held.tile([P, S], F32, name="last_frac", align_bytes=64)
+            else:
+                st["f"] = ring.tile([P, S], F32, name="frac")
+            for half in range(2):
+                nc.vector.tensor_scalar(turns[:, halfcols(half)], st["ph"][half][:], 1.0 / TWO_PI, None, ALU.mult)
             for half in range(2):
                 nc.vector.scalar_tensor_tensor(
-                    st["f"][:, halfcols(half)], st["ph"][half][:], 1.0 / TWO_PI, st["k"][:, halfcols(half)], ALU.mult, ALU.subtract
+                    st["f"][:, halfcols(half)], st["ph"][half][:], 1.0 / TWO_PI, turns[:, halfcols(half)], ALU.mult, ALU.subtract
                 )
-            nc.scalar.activation(st["f"][:], st["f"][:], ACT.Sin, bias=-math.pi, scale=-TWO_PI)
+            nc.scalar.activation(st["f"][:], st["f"][:], ACT.Sin, scale=TWO_PI)
 
         def larger(i):
             st = state[i]
@@ -178,108 +172,160 @@ def tile_list_shellac_click_segments_kernel(
                 nc.vector.tensor_tensor(st["m"][:, halfcols(half)], st["rt"][half][:], st["m"][:, halfcols(half)], ALU.max)
 
         def wobble(i):
-            b, t = divmod(i, PACK)
             st = state[i]
-            nc.vector.scalar_tensor_tensor(st["f"][:], st["f"][:], gain_sb[:, b, t : t + 1], speeds[i][:], ALU.mult, ALU.mult)
+            if i == TILES - 1:
+                st["w"] = st["f"]
+                nc.vector.tensor_tensor(st["w"][:], st["f"][:], speeds[i][:], ALU.mult)
+            else:
+                st["w"] = held.tile([P, S], F32, name="wobble", align_bytes=64)
+                nc.gpsimd.tensor_tensor(st["w"][:], st["f"][:], speeds[i][:], ALU.mult)
 
         def feature(i):
-            b, t = divmod(i, PACK)
             st = state[i]
-            hs[i] = held.tile([P, S], F32, name="h%d" % i)
-            nc.vector.scalar_tensor_tensor(hs[i][:], st["m"][:], gain_sb[:, b, t : t + 1], st["f"][:], ALU.mult, ALU.add)
+            us[i] = held.tile([P, S], F32, name="u%d" % i)
+            nc.vector.tensor_tensor(us[i][:], st["m"][:], st["w"][:], ALU.add)
 
-        def pick(i):
-            b, t = divmod(i, PACK)
-            if t == 0:
-                picked[b] = ring.tile([P, PACK, NP], BF16, name="picked")
-            nc.vector.tensor_copy(picked[b][:, t, :], hs[i][:].indirect(p1[:]))
-
-        def weave_picked(b, engine_copy):
-            woven = ring.tile([P, NP * PACK], BF16, name="woven", bufs=3, align_bytes=64)
-            engine_copy(
-                out=woven[:].rearrange("p (c i t) -> p c t i", i=4, t=PACK),
-                in_=picked[b][:].rearrange("p t (c i) -> p c t i", i=4),
+        def pick(i, m0, m1):
+            b, c = divmod(i, PACK)
+            if b not in turned:
+                turned[b] = ring.tile([P, PACK, 2, P], F32, name="turned")
+            width = m1 - m0
+            got = ring.tile([P, width], F32, name="got")
+            nc.vector.tensor_copy(got[:], us[i][:].indirect(p1[:, m0 // 16 : m1 // 16]))
+            x = ring.tile([P, width], BF16, name="x")
+            nc.scalar.activation(x[:], got[:], ACT.Copy, scale=factors[:, i : i + 1])
+            bank = psum.tile([P, width // P, P], BF16, name="turn")
+            for mt in range(width // P):
+                nc.tensor.transpose(bank[:, mt, :], x[:, mt * P : (mt + 1) * P], ident16[:])
+            nc.scalar.copy(
+                out=turned[b][:, m0 // P : m1 // P, :, 32 * c : 32 * (c + 1)],
+                in_=bank[:].bitcast(F32).rearrange("m t (q u) -> m t u q", u=2),
             )
-            return woven
 
-        extra = {}
-        products(0)
+        def turn_back(b, half):
+            bank = psum.tile([P, 2, 2, P], F32, name="turn")
+            for mt in range(2):
+                for u in range(2):
+                    nc.tensor.transpose(bank[:, mt, u, :], turned[b][:, 2 * half + mt, u, :], ident[:])
+            xw = ring.tile([P, HALF * PACK], BF16, name="xwoven", bufs=4, align_bytes=64)
+            nc.scalar.copy(
+                out=xw[:].bitcast(F32).rearrange("p (t m u) -> p t m u", t=2, u=2),
+                in_=bank[:].rearrange("p t u m -> p t m u"),
+            )
+            return xw
+
+        def quantise_x(b, half, xw):
+            if b not in xq:
+                xq[b] = (
+                    held.tile([P, NP], U32, name=("wobble", "codes_x1")[b], align_bytes=64),
+                    held.tile([P, NP], U8, name="scales_x%d" % b, align_bytes=64),
+                )
+            cols = slice(half * HALF, (half + 1) * HALF)
+            nc.vector.quantize_mx(out=xq[b][0][:, cols].bitcast(FP8X4), scales=xq[b][1][:, cols], in_=xw[:])
+
+        def weave_second(a, b, part, name):
+            if (a, b) not in woven:
+                woven[a, b] = ring.tile([P, PASS * PACK], BF16, name=name, align_bytes=64)
+            weave(woven[a, b], raw5[a, b], part * CHUNK, (part + 1) * CHUNK)
+
+        phase_products(0)
+        pair_products(0)
         for i in range(TILES + 1):
             if i < TILES:
-                turns(i)
-            if i > 0:
-                wobble(i - 1)
-            if i == 1:
-                speeds[7] = load_speed(7)
-                for a, b in ((0, 0), (1, 0), (0, 1), (1, 1)):
-                    raw5[a, b] = load_weight(w5, a, b)
-                nc.sync.dma_start(out=skip_sb[:], in_=skip.rearrange("(b p t) -> p b t", p=P, t=PACK))
-                for q in range(4):
-                    nc.sync.dma_start(out=wgo_sb[32 * q : 32 * (q + 1), :, :], in_=wgo.rearrange("(p t) m -> p t m", t=PACK))
+                sine(i)
             if i < TILES:
-                fraction(i)
+                larger(i)
+            if i % 2 == 1 and i + 1 < TILES:
+                q1[(i + 1) // 2] = quantise(woven["w1"], CHUNK, "w1_%d" % ((i + 1) // 2))
+                q3[(i + 1) // 2] = quantise(woven["w3"], CHUNK, "w3_%d" % ((i + 1) // 2))
+            if i + 1 < TILES:
+                phase_products(i + 1)
+                pair_products(i + 1)
+            if i == 0:
+                spread = psum.tile([P, P], F32, name="turn")
+                nc.tensor.transpose(spread[:], rows[:], ident[:])
+                nc.scalar.copy(out=factors[:, 0 : 2 * TILES], in_=spread[:, 0 : 2 * TILES])
+                nc.gpsimd.tensor_tensor(factors[:, 2 * TILES :], factors[:, 0:TILES], factors[:, TILES : 2 * TILES], ALU.mult)
+            if i > 1:
+                pick(i - 2, 0, NP)
             if i > 0:
                 feature(i - 1)
             if i < TILES:
-                larger(i)
+                wobble(i)
+            if i % 2 == 0 and i + 2 < TILES:
+                woven["w1"] = weave_first(raw1[i // 2 + 1])
+                woven["w3"] = weave_first(raw3[i // 2 + 1])
             if i == 0:
-                extra["w1"] = weave_weight(raw1[1])
-            if i == 1:
-                extra["w3"] = weave_weight(raw3[1])
-                q1[1] = quantise(extra["w1"], "w1_1")
-            if i == 2:
-                q3[1] = quantise(extra["w3"], "w3_1")
-                woven5[0, 0] = weave_weight(raw5[0, 0])
-            if i == 3:
-                q5[0, 0] = quantise(woven5[0, 0], "w5_00")
-                woven5[1, 0] = weave_weight(raw5[1, 0])
-            if i == 4:
-                q5[1, 0] = quantise(woven5[1, 0], "w5_10")
-                deal(w4s[:].rearrange("p a c -> p (a c)"), w4s_raw[:].rearrange("p a c -> p (a c)"))
+                for a in range(2):
+                    raw5[a, 0] = load_weight(w5, a, 0, PASS, "raw5", 2)
+                for q in range(4):
+                    nc.sync.dma_start(
+                        out=w4s[32 * q : 32 * q + 4, :, :].bitcast(I32),
+                        in_=w4_scales[:, 4 * q : 4 * q + 4, :].rearrange("a r c -> r a c").bitcast(I32),
+                    )
+                nc.sync.dma_start(out=w4w[:].bitcast(I32), in_=w4_words.rearrange("a p c -> p a c").bitcast(I32))
+                nc.sync.dma_start(out=wgo_sb[:], in_=wgo)
+            if i + 4 < TILES:
+                speeds[i + 4] = load_speed(i + 4)
+            if i in (1, 3, 5, 6):
+                step = (1, 3, 5, 6).index(i)
+                weave_second(step // 2, 0, step % 2, "woven5")
+            if i in (3, 6):
+                raw5[i // 6, 1] = load_weight(w5, i // 6, PASS, PASS, "raw5", 2)
             if i == 5:
-                extra["x0"] = weave_picked(0, nc.scalar.copy)
-            if i == 6:
-                xq[0] = quantise(extra["x0"], "x0")
-                woven5[0, 1] = weave_weight(raw5[0, 1])
-            if i == 7:
-                woven5[1, 1] = weave_weight(raw5[1, 1])
-            if i + 1 < TILES:
-                products(i + 1)
-            if i > 0:
-                pick(i - 1)
+                woven["x0"] = [turn_back(0, half) for half in range(2)]
 
-        extra["x1"] = weave_picked(1, nc.vector.tensor_copy)
-        q5[0, 1] = quantise(woven5[0, 1], "w5_01")
-        xq[1] = quantise(extra["x1"], "x1")
-        q5[1, 1] = quantise(woven5[1, 1], "w5_11")
+        for half in range(2):
+            quantise_x(0, half, woven["x0"][half])
+        last = TILES - 1
+        for half in range(2):
+            pick(last, half * HALF, (half + 1) * HALF)
+        woven["x1"] = [turn_back(1, half) for half in range(2)]
+        q5[0, 0] = quantise(woven[0, 0], PASS, "w5_00", "last_larger")
+        q5[1, 0] = quantise(woven[1, 0], PASS, "w5_10", "last_frac")
 
-        second = {}
+        ys, pages = {}, {}
 
-        def second_products(i):
+        def second_products(i, m0, m1):
             b, t = divmod(i, PACK)
-            cols = slice(t * P, (t + 1) * P)
-            wide = slice(i * P, (i + 1) * P)
-            y1 = psum.tile([P, NP], F32, name="phase", bufs=4)
+            cols, wide, ms = slice(t * P, (t + 1) * P), slice(i * P, (i + 1) * P), slice(m0, m1)
+            y1 = psum.tile([P, m1 - m0], F32, name="phase" if i == 0 else "left")
             for a in range(2):
-                mx(y1[:], w4w[:, a, wide].bitcast(FP4X4), w4s[:, a, wide], xq[a][0][:].bitcast(FP8X4), xq[a][1][:], a == 0, a == 1)
-            y2 = psum.tile([P, NP], F32, name="right")
+                mx(y1[:], w4w[:, a, wide].bitcast(FP4X4), w4s[:, a, wide], xq[a][0][:, ms].bitcast(FP8X4), xq[a][1][:, ms], a == 0, a == 1)
+            y2 = psum.tile([P, m1 - m0], F32, name="right")
             for a in range(2):
-                mx(y2[:], q5[a, b][0][:, cols].bitcast(FP8X4), q5[a, b][1][:, cols], xq[a][0][:].bitcast(FP8X4), xq[a][1][:], a == 0, a == 1)
-            y = ring.tile([P, NP], F32, name="y", bufs=3)
+                mx(y2[:], q5[a, b][0][:, cols].bitcast(FP8X4), q5[a, b][1][:, cols], xq[a][0][:, ms].bitcast(FP8X4), xq[a][1][:, ms], a == 0, a == 1)
+            if i == 0:
+                y = ring.tile([P, m1 - m0], F32, name="woven5", align_bytes=64)
+            else:
+                y = ring.tile([P, m1 - m0], F32, name="y", bufs=3)
             nc.scalar.copy(out=y[:], in_=y1[:])
-            page = ring.tile([P, S], F32, name="row", bufs=7)
-            nc.scalar.activation(page[:], hs[i][:], ACT.Copy, scale=skip_sb[:, b, t : t + 1])
             nc.vector.tensor_tensor(y[:], y2[:], y[:], ALU.max)
-            second[i] = (y, page)
+            ys[i, m0] = y
 
-        def put(i):
-            b, t = divmod(i, PACK)
-            y, page = second[i]
-            nc.vector.tensor_tensor(page[:].indirect(p1[:]), y[:], wgo_sb[:, t, :], ALU.mult)
-            nc.sync.dma_start(out=out[b * PASS : (b + 1) * PASS, :].rearrange("(p t) j -> p t j", t=PACK)[:, t, :], in_=page[:])
+        def make_page(i):
+            pages[i] = ring.tile([P, S], F32, name="page", bufs=3)
+            nc.scalar.activation(pages[i][:], us[i][:], ACT.Copy, scale=factors[:, 2 * TILES + i : 2 * TILES + i + 1])
 
-        second_products(0)
+        def put(i, m0, m1):
+            nc.vector.tensor_tensor(pages[i][:].indirect(p1[:, m0 // 16 : m1 // 16]), ys[i, m0][:], wgo_sb[:, m0:m1], ALU.mult)
+
+        make_page(0)
+        for half in range(2):
+            quantise_x(1, half, woven["x1"][half])
+            second_products(0, half * HALF, (half + 1) * HALF)
+        put(0, 0, HALF)
         for i in range(TILES):
             if i + 1 < TILES:
-                second_products(i + 1)
-            put(i)
+                second_products(i + 1, 0, NP)
+            if i == 0:
+                put(0, HALF, NP)
+            else:
+                make_page(i)
+                put(i, 0, NP)
+            nc.sync.dma_start(out=out[i * P : (i + 1) * P, :], in_=pages[i][:])
+            if i < 2:
+                for part in range(2):
+                    weave_second(i, 1, part, "woven5")
+            if i in (1, 2):
+                q5[i - 1, 1] = quantise(woven[i - 1, 1], PASS, "w5_%d1" % (i - 1))

@@ -51,7 +51,8 @@ def tile_list_shellac_click_segments_kernel(
         ident = held.tile([P, P], F32, name="ident")
         ident16 = held.tile([P, P], BF16, name="ident16")
 
-        nc.vector.memset(tabs[:].bitcast(I32), 0)
+        nc.gpsimd.memset(tabs[:, 0 : T // 2].bitcast(I32), 0)
+        nc.vector.memset(tabs[:, T // 2 :].bitcast(I32), 0)
         nc.vector.memset(w2s[:].bitcast(I32), 0)
         nc.vector.memset(w4s[:].rearrange("p a c -> p (a c)").bitcast(I32), 0)
         nc.gpsimd.memset(rows[:], 0.0)
@@ -64,7 +65,7 @@ def tile_list_shellac_click_segments_kernel(
             return raw
 
         def load_first(w, c):
-            return load_weight(w, 0, c * CHUNK, CHUNK, "raw", 4)
+            return load_weight(w, 0, c * CHUNK, CHUNK, "raw", 3)
 
         def weave(woven, raw, c0, c1):
             nc.scalar.copy(
@@ -77,8 +78,8 @@ def tile_list_shellac_click_segments_kernel(
             weave(woven, raw, 0, CHUNK)
             return woven
 
-        def quantise(woven, width, label, slot=None):
-            codes = held.tile([P, width], U32, name=slot or "codes_" + label, align_bytes=64)
+        def quantise(woven, width, label):
+            codes = held.tile([P, width], U32, name="codes_" + label, align_bytes=64)
             scales = held.tile([P, width], U8, name="scales_" + label, align_bytes=64)
             nc.vector.quantize_mx(out=codes[:].bitcast(FP8X4), scales=scales[:], in_=woven[:])
             return codes, scales
@@ -93,9 +94,9 @@ def tile_list_shellac_click_segments_kernel(
         nc.sync.dma_start(idx[:], offs)
         nc.sync.dma_start(p1[:], pos1)
         nc.sync.dma_start(out=rows[0:TILES, :], in_=gain.rearrange("(i p) -> i p", p=P))
+        nc.sync.dma_start(out=tabw[:].bitcast(I32), in_=tab_words[0].rearrange("p t i -> p (t i)").bitcast(I32))
         raw1 = {0: load_first(w1, 0)}
         nc.sync.dma_start(out=w2w[:].bitcast(I32), in_=w2_words[0].bitcast(I32))
-        nc.sync.dma_start(out=tabw[:].bitcast(I32), in_=tab_words[0].rearrange("p t i -> p (t i)").bitcast(I32))
         for q in range(4):
             nc.sync.dma_start(out=w2s[32 * q : 32 * q + 4, :].bitcast(I32), in_=w2_scales[0, 4 * q : 4 * q + 4, :].bitcast(I32))
         raw3 = {0: load_first(w3, 0)}
@@ -111,11 +112,11 @@ def tile_list_shellac_click_segments_kernel(
             sbytes = held.tile([P, BANK], U8, name="vs%d" % half, align_bytes=64)
             nc.vector.tensor_copy(sbytes[:], tabs[:].indirect(idx[:, half * (BANK // 16) : (half + 1) * (BANK // 16)]))
             vs.append(sbytes)
-        q1 = {0: quantise(weave_first(raw1[0]), CHUNK, "w1_0")}
         for half in range(2):
             words = held.tile([P, BANK], U32, name="vw%d" % half, align_bytes=64)
             nc.vector.tensor_copy(words[:], tabw[:].indirect(idx[:, half * (BANK // 16) : (half + 1) * (BANK // 16)]))
             vw.append(words)
+        q1 = {0: quantise(weave_first(raw1[0]), CHUNK, "w1_0")}
         q3 = {0: quantise(weave_first(raw3[0]), CHUNK, "w3_0")}
 
         q5, raw5, woven, xq, turned, state, us = {}, {}, {}, {}, {}, {}, {}
@@ -175,7 +176,7 @@ def tile_list_shellac_click_segments_kernel(
             st = state[i]
             if i == TILES - 1:
                 st["w"] = st["f"]
-                nc.vector.tensor_tensor(st["w"][:], st["f"][:], speeds[i][:], ALU.mult)
+                nc.vector.scalar_tensor_tensor(st["w"][:], st["f"][:], factors[:, i : i + 1], speeds[i][:], ALU.mult, ALU.mult)
             else:
                 st["w"] = held.tile([P, S], F32, name="wobble", align_bytes=64)
                 nc.gpsimd.tensor_tensor(st["w"][:], st["f"][:], speeds[i][:], ALU.mult)
@@ -183,17 +184,23 @@ def tile_list_shellac_click_segments_kernel(
         def feature(i):
             st = state[i]
             us[i] = held.tile([P, S], F32, name="u%d" % i)
-            nc.vector.tensor_tensor(us[i][:], st["m"][:], st["w"][:], ALU.add)
+            if i == TILES - 1:
+                nc.vector.scalar_tensor_tensor(us[i][:], st["m"][:], factors[:, i : i + 1], st["w"][:], ALU.mult, ALU.add)
+            else:
+                nc.vector.tensor_tensor(us[i][:], st["m"][:], st["w"][:], ALU.add)
 
         def pick(i, m0, m1):
             b, c = divmod(i, PACK)
             if b not in turned:
                 turned[b] = ring.tile([P, PACK, 2, P], F32, name="turned")
             width = m1 - m0
-            got = ring.tile([P, width], F32, name="got")
-            nc.vector.tensor_copy(got[:], us[i][:].indirect(p1[:, m0 // 16 : m1 // 16]))
             x = ring.tile([P, width], BF16, name="x")
-            nc.scalar.activation(x[:], got[:], ACT.Copy, scale=factors[:, i : i + 1])
+            if i == TILES - 1:
+                nc.vector.tensor_copy(x[:], us[i][:].indirect(p1[:, m0 // 16 : m1 // 16]))
+            else:
+                got = ring.tile([P, width], F32, name="got")
+                nc.vector.tensor_copy(got[:], us[i][:].indirect(p1[:, m0 // 16 : m1 // 16]))
+                nc.scalar.activation(x[:], got[:], ACT.Copy, scale=factors[:, i : i + 1])
             bank = psum.tile([P, width // P, P], BF16, name="turn")
             for mt in range(width // P):
                 nc.tensor.transpose(bank[:, mt, :], x[:, mt * P : (mt + 1) * P], ident16[:])
@@ -217,15 +224,15 @@ def tile_list_shellac_click_segments_kernel(
         def quantise_x(b, half, xw):
             if b not in xq:
                 xq[b] = (
-                    held.tile([P, NP], U32, name=("wobble", "codes_x1")[b], align_bytes=64),
+                    held.tile([P, NP], U32, name=("last_frac", "codes_x1")[b], align_bytes=64),
                     held.tile([P, NP], U8, name="scales_x%d" % b, align_bytes=64),
                 )
             cols = slice(half * HALF, (half + 1) * HALF)
             nc.vector.quantize_mx(out=xq[b][0][:, cols].bitcast(FP8X4), scales=xq[b][1][:, cols], in_=xw[:])
 
-        def weave_second(a, b, part, name):
+        def weave_second(a, b, part):
             if (a, b) not in woven:
-                woven[a, b] = ring.tile([P, PASS * PACK], BF16, name=name, align_bytes=64)
+                woven[a, b] = held.tile([P, PASS * PACK], BF16, name="woven5_%d%d" % (a, b), align_bytes=64)
             weave(woven[a, b], raw5[a, b], part * CHUNK, (part + 1) * CHUNK)
 
         phase_products(0)
@@ -268,21 +275,29 @@ def tile_list_shellac_click_segments_kernel(
             if i + 4 < TILES:
                 speeds[i + 4] = load_speed(i + 4)
             if i in (1, 3, 5, 6):
-                step = (1, 3, 5, 6).index(i)
-                weave_second(step // 2, 0, step % 2, "woven5")
-            if i in (3, 6):
-                raw5[i // 6, 1] = load_weight(w5, i // 6, PASS, PASS, "raw5", 2)
+                b, a = divmod((1, 3, 5, 6).index(i), 2)
+                for part in range(2):
+                    weave_second(a, b, part)
+                if b == 0:
+                    raw5[a, 1] = load_weight(w5, a, PASS, PASS, "raw5", 2)
             if i == 5:
                 woven["x0"] = [turn_back(0, half) for half in range(2)]
 
-        for half in range(2):
-            quantise_x(0, half, woven["x0"][half])
         last = TILES - 1
         for half in range(2):
             pick(last, half * HALF, (half + 1) * HALF)
         woven["x1"] = [turn_back(1, half) for half in range(2)]
-        q5[0, 0] = quantise(woven[0, 0], PASS, "w5_00", "last_larger")
-        q5[1, 0] = quantise(woven[1, 0], PASS, "w5_10", "last_frac")
+        for half in range(2):
+            quantise_x(0, half, woven["x0"][half])
+        codes5 = held.tile([P, 4, PASS], U32, name="last_larger", align_bytes=64)
+
+        def quantise_second(a, b):
+            scales5 = held.tile([P, PASS], U8, name="scales_w5_%d%d" % (a, b), align_bytes=64)
+            nc.vector.quantize_mx(out=codes5[:, 2 * b + a, :].bitcast(FP8X4), scales=scales5[:], in_=woven[a, b][:])
+            q5[a, b] = (codes5[:, 2 * b + a, :], scales5)
+
+        for a in range(2):
+            quantise_second(a, 0)
 
         ys, pages = {}, {}
 
@@ -296,16 +311,17 @@ def tile_list_shellac_click_segments_kernel(
             for a in range(2):
                 mx(y2[:], q5[a, b][0][:, cols].bitcast(FP8X4), q5[a, b][1][:, cols], xq[a][0][:, ms].bitcast(FP8X4), xq[a][1][:, ms], a == 0, a == 1)
             if i == 0:
-                y = ring.tile([P, m1 - m0], F32, name="woven5", align_bytes=64)
+                y = held.tile([P, m1 - m0], F32, name="page%d" % (1 + m0 // HALF))
             else:
-                y = ring.tile([P, m1 - m0], F32, name="y", bufs=3)
+                y = ring.tile([P, m1 - m0], F32, name="y", bufs=4)
             nc.scalar.copy(out=y[:], in_=y1[:])
             nc.vector.tensor_tensor(y[:], y2[:], y[:], ALU.max)
             ys[i, m0] = y
 
         def make_page(i):
-            pages[i] = ring.tile([P, S], F32, name="page", bufs=3)
-            nc.scalar.activation(pages[i][:], us[i][:], ACT.Copy, scale=factors[:, 2 * TILES + i : 2 * TILES + i + 1])
+            pages[i] = held.tile([P, S], F32, name="page%d" % (i % 3))
+            col = TILES + i if i == TILES - 1 else 2 * TILES + i
+            nc.scalar.activation(pages[i][:], us[i][:], ACT.Copy, scale=factors[:, col : col + 1])
 
         def put(i, m0, m1):
             nc.vector.tensor_tensor(pages[i][:].indirect(p1[:, m0 // 16 : m1 // 16]), ys[i, m0][:], wgo_sb[:, m0:m1], ALU.mult)
@@ -324,8 +340,5 @@ def tile_list_shellac_click_segments_kernel(
                 make_page(i)
                 put(i, 0, NP)
             nc.sync.dma_start(out=out[i * P : (i + 1) * P, :], in_=pages[i][:])
-            if i < 2:
-                for part in range(2):
-                    weave_second(i, 1, part, "woven5")
             if i in (1, 2):
-                q5[i - 1, 1] = quantise(woven[i - 1, 1], PASS, "w5_%d1" % (i - 1))
+                quantise_second(i - 1, 1)

import math
from contextlib import ExitStack

import concourse.mybir as mybir
from concourse.masks import make_identity

K, T, S, H, NP = 512, 4096, 1024, 1024, 512
FLOPS = 2 * (3 * K * H * S + 2 * H * H * NP)

F32 = mybir.dt.float32
BF16 = mybir.dt.bfloat16
I32 = mybir.dt.int32
U32 = mybir.dt.uint32
U16 = mybir.dt.uint16
U8 = mybir.dt.uint8
FP8X4 = mybir.dt.float8_e4m3fn_x4
FP4X4 = mybir.dt.float4_e2m1fn_x4
ALU = mybir.AluOpType
ACT = mybir.ActivationFunctionType

P = 128
PACK = 4
PASS = P * PACK
BANK = 512
TILES = H // P
CHUNK = 256
HALF = NP // 2
TWO_PI = 2.0 * math.pi


def tile_list_shellac_click_segments_kernel(
    tc, tab_words, tab_scales, offs, pos1, w1, w2_words, w2_scales, w3, speed, gain, w4_words, w4_scales, w5, skip, wgo, out
):
    nc = tc.nc
    with ExitStack() as ctx:
        held = ctx.enter_context(tc.tile_pool(name="held", bufs=1))
        ring = ctx.enter_context(tc.tile_pool(name="ring", bufs=2))
        psum = ctx.enter_context(tc.psum_pool(name="psum", bufs=2))

        idx = held.tile([P, S // 16], U16, name="idx")
        p1 = held.tile([P, NP // 16], U16, name="p1")
        tabw = held.tile([P, T], U32, name="tabw", align_bytes=64)
        tabs = held.tile([P, T], U8, name="tabs", align_bytes=64)
        w2w = held.tile([P, H], U16, name="w2w", align_bytes=64)
        w2s = held.tile([P, H], U8, name="w2s", align_bytes=64)
        w4w = held.tile([P, 2, H], U16, name="w4w", align_bytes=64)
        w4s = held.tile([P, 2, H], U8, name="w4s", align_bytes=64)
        wgo_sb = held.tile([P, NP], F32, name="wgo_sb")
        rows = held.tile([P, P], F32, name="rows")
        factors = held.tile([P, 3 * TILES], F32, name="factors")
        ident = held.tile([P, P], F32, name="ident")
        ident16 = held.tile([P, P], BF16, name="ident16")

        nc.gpsimd.memset(tabs[:, 0 : T // 2].bitcast(I32), 0)
        nc.vector.memset(tabs[:, T // 2 :].bitcast(I32), 0)
        nc.vector.memset(w2s[:].bitcast(I32), 0)
        nc.vector.memset(w4s[:].rearrange("p a c -> p (a c)").bitcast(I32), 0)
        nc.gpsimd.memset(rows[:], 0.0)
        make_identity(nc, ident[:])
        make_identity(nc, ident16[:])

        def load_weight(w, a, c0, width, name, bufs):
            raw = ring.tile([P, PACK, width], F32, name=name, bufs=bufs)
            nc.sync.dma_start(out=raw[:], in_=w[a * PASS : (a + 1) * PASS, c0 : c0 + width].rearrange("(p j) c -> p j c", j=PACK))
            return raw

        def load_first(w, c):
            return load_weight(w, 0, c * CHUNK, CHUNK, "raw", 3)

        def weave(woven, raw, c0, c1):
            nc.scalar.copy(
                out=woven[:].rearrange("p (c i j) -> p c j i", i=4, j=PACK)[:, c0 // 4 : c1 // 4],
                in_=raw[:].rearrange("p j (c i) -> p c j i", i=4)[:, c0 // 4 : c1 // 4],
            )

        def weave_first(raw):
            woven = ring.tile([P, CHUNK * PACK], BF16, name="woven", bufs=3, align_bytes=64)
            weave(woven, raw, 0, CHUNK)
            return woven

        def quantise(woven, width, label):
            codes = held.tile([P, width], U32, name="codes_" + label, align_bytes=64)
            scales = held.tile([P, width], U8, name="scales_" + label, align_bytes=64)
            nc.vector.quantize_mx(out=codes[:].bitcast(FP8X4), scales=scales[:], in_=woven[:])
            return codes, scales

        def load_speed(i):
            sp = ring.tile([P, S], F32, name="speed", bufs=4)
            nc.sync.dma_start(out=sp[:], in_=speed[i * P : (i + 1) * P, :])
            return sp

        for q in range(4):
            nc.sync.dma_start(out=tabs[32 * q : 32 * q + 4, :].bitcast(I32), in_=tab_scales[0, 4 * q : 4 * q + 4, :].bitcast(I32))
        nc.sync.dma_start(idx[:], offs)
        nc.sync.dma_start(p1[:], pos1)
        nc.sync.dma_start(out=rows[0:TILES, :], in_=gain.rearrange("(i p) -> i p", p=P))
        nc.sync.dma_start(out=tabw[:].bitcast(I32), in_=tab_words[0].rearrange("p t i -> p (t i)").bitcast(I32))
        raw1 = {0: load_first(w1, 0)}
        nc.sync.dma_start(out=w2w[:].bitcast(I32), in_=w2_words[0].bitcast(I32))
        for q in range(4):
            nc.sync.dma_start(out=w2s[32 * q : 32 * q + 4, :].bitcast(I32), in_=w2_scales[0, 4 * q : 4 * q + 4, :].bitcast(I32))
        raw3 = {0: load_first(w3, 0)}
        speeds = {0: load_speed(0)}
        nc.sync.dma_start(out=rows[TILES : 2 * TILES, :], in_=skip.rearrange("(i p) -> i p", p=P))
        for c in range(1, 4):
            raw1[c] = load_first(w1, c)
            raw3[c] = load_first(w3, c)
            speeds[c] = load_speed(c)

        vw, vs = [], []
        for half in range(2):
            sbytes = held.tile([P, BANK], U8, name="vs%d" % half, align_bytes=64)
            nc.vector.tensor_copy(sbytes[:], tabs[:].indirect(idx[:, half * (BANK // 16) : (half + 1) * (BANK // 16)]))
            vs.append(sbytes)
        for half in range(2):
            words = held.tile([P, BANK], U32, name="vw%d" % half, align_bytes=64)
            nc.vector.tensor_copy(words[:], tabw[:].indirect(idx[:, half * (BANK // 16) : (half + 1) * (BANK // 16)]))
            vw.append(words)
        q1 = {0: quantise(weave_first(raw1[0]), CHUNK, "w1_0")}
        q3 = {0: quantise(weave_first(raw3[0]), CHUNK, "w3_0")}

        q5, raw5, woven, xq, turned, state, us = {}, {}, {}, {}, {}, {}, {}

        def mx(acc, lw, ls, rw, rs, start, stop):
            nc.tensor.matmul_mx(out=acc, lhsT=lw, lhsT_scale=ls, rhs=rw, rhs_scale=rs, start=start, stop=stop)

        def halfcols(half):
            return slice(half * BANK, (half + 1) * BANK)

        def phase_products(i):
            c, cols = i // 2, slice((i % 2) * P, (i % 2 + 1) * P)
            state[i] = {"ph": []}
            for half in range(2):
                acc = psum.tile([P, BANK], F32, name="phase")
                mx(acc[:], q1[c][0][:, cols].bitcast(FP8X4), q1[c][1][:, cols], vw[half][:].bitcast(FP8X4), vs[half][:], True, True)
                state[i]["ph"].append(acc)

        def pair_products(i):
            c, cols, wide = i // 2, slice((i % 2) * P, (i % 2 + 1) * P), slice(i * P, (i + 1) * P)
            st = state[i]
            st["rt"] = []
            if i == TILES - 1:
                st["m"] = held.tile([P, S], F32, name="last_larger", align_bytes=64)
            else:
                st["m"] = ring.tile([P, S], F32, name="larger", bufs=3)
            for half in range(2):
                lf = psum.tile([P, BANK], F32, name="left")
                mx(lf[:], w2w[:, wide].bitcast(FP4X4), w2s[:, wide], vw[half][:].bitcast(FP8X4), vs[half][:], True, True)
                nc.scalar.copy(out=st["m"][:, halfcols(half)], in_=lf[:])
            for half in range(2):
                acc = psum.tile([P, BANK], F32, name="right")
                mx(acc[:], q3[c][0][:, cols].bitcast(FP8X4), q3[c][1][:, cols], vw[half][:].bitcast(FP8X4), vs[half][:], True, True)
                st["rt"].append(acc)

        def sine(i):
            st = state[i]
            turns = ring.tile([P, S], I32, name="turns", bufs=1)
            if i == TILES - 1:
                st["f"] = held.tile([P, S], F32, name="last_frac", align_bytes=64)
            else:
                st["f"] = ring.tile([P, S], F32, name="frac")
            for half in range(2):
                nc.vector.tensor_scalar(turns[:, halfcols(half)], st["ph"][half][:], 1.0 / TWO_PI, None, ALU.mult)
            for half in range(2):
                nc.vector.scalar_tensor_tensor(
                    st["f"][:, halfcols(half)], st["ph"][half][:], 1.0 / TWO_PI, turns[:, halfcols(half)], ALU.mult, ALU.subtract
                )
            nc.scalar.activation(st["f"][:], st["f"][:], ACT.Sin, scale=TWO_PI)

        def larger(i):
            st = state[i]
            for half in range(2):
                nc.vector.tensor_tensor(st["m"][:, halfcols(half)], st["rt"][half][:], st["m"][:, halfcols(half)], ALU.max)

        def wobble(i):
            st = state[i]
            if i == TILES - 1:
                st["w"] = st["f"]
                nc.vector.scalar_tensor_tensor(st["w"][:], st["f"][:], factors[:, i : i + 1], speeds[i][:], ALU.mult, ALU.mult)
            else:
                st["w"] = held.tile([P, S], F32, name="wobble", align_bytes=64)
                nc.gpsimd.tensor_tensor(st["w"][:], st["f"][:], speeds[i][:], ALU.mult)

        def feature(i):
            st = state[i]
            us[i] = held.tile([P, S], F32, name="u%d" % i)
            if i == TILES - 1:
                nc.vector.scalar_tensor_tensor(us[i][:], st["m"][:], factors[:, i : i + 1], st["w"][:], ALU.mult, ALU.add)
            else:
                nc.vector.tensor_tensor(us[i][:], st["m"][:], st["w"][:], ALU.add)

        def pick(i, m0, m1):
            b, c = divmod(i, PACK)
            if b not in turned:
                turned[b] = ring.tile([P, PACK, 2, P], F32, name="turned")
            width = m1 - m0
            x = ring.tile([P, width], BF16, name="x")
            if i == TILES - 1:
                nc.vector.tensor_copy(x[:], us[i][:].indirect(p1[:, m0 // 16 : m1 // 16]))
            else:
                got = ring.tile([P, width], F32, name="got")
                nc.vector.tensor_copy(got[:], us[i][:].indirect(p1[:, m0 // 16 : m1 // 16]))
                nc.scalar.activation(x[:], got[:], ACT.Copy, scale=factors[:, i : i + 1])
            bank = psum.tile([P, width // P, P], BF16, name="turn")
            for mt in range(width // P):
                nc.tensor.transpose(bank[:, mt, :], x[:, mt * P : (mt + 1) * P], ident16[:])
            nc.scalar.copy(
                out=turned[b][:, m0 // P : m1 // P, :, 32 * c : 32 * (c + 1)],
                in_=bank[:].bitcast(F32).rearrange("m t (q u) -> m t u q", u=2),
            )

        def turn_back(b, half):
            bank = psum.tile([P, 2, 2, P], F32, name="turn")
            for mt in range(2):
                for u in range(2):
                    nc.tensor.transpose(bank[:, mt, u, :], turned[b][:, 2 * half + mt, u, :], ident[:])
            xw = ring.tile([P, HALF * PACK], BF16, name="xwoven", bufs=4, align_bytes=64)
            nc.scalar.copy(
                out=xw[:].bitcast(F32).rearrange("p (t m u) -> p t m u", t=2, u=2),
                in_=bank[:].rearrange("p t u m -> p t m u"),
            )
            return xw

        def quantise_x(b, half, xw):
            if b not in xq:
                xq[b] = (
                    held.tile([P, NP], U32, name=("last_frac", "codes_x1")[b], align_bytes=64),
                    held.tile([P, NP], U8, name="scales_x%d" % b, align_bytes=64),
                )
            cols = slice(half * HALF, (half + 1) * HALF)
            nc.vector.quantize_mx(out=xq[b][0][:, cols].bitcast(FP8X4), scales=xq[b][1][:, cols], in_=xw[:])

        def weave_second(a, b, part):
            if (a, b) not in woven:
                woven[a, b] = held.tile([P, PASS * PACK], BF16, name="woven5_%d%d" % (a, b), align_bytes=64)
            weave(woven[a, b], raw5[a, b], part * CHUNK, (part + 1) * CHUNK)

        phase_products(0)
        pair_products(0)
        for i in range(TILES + 1):
            if i < TILES:
                sine(i)
            if i < TILES:
                larger(i)
            if i % 2 == 1 and i + 1 < TILES:
                q1[(i + 1) // 2] = quantise(woven["w1"], CHUNK, "w1_%d" % ((i + 1) // 2))
                q3[(i + 1) // 2] = quantise(woven["w3"], CHUNK, "w3_%d" % ((i + 1) // 2))
            if i + 1 < TILES:
                phase_products(i + 1)
                pair_products(i + 1)
            if i == 0:
                spread = psum.tile([P, P], F32, name="turn")
                nc.tensor.transpose(spread[:], rows[:], ident[:])
                nc.scalar.copy(out=factors[:, 0 : 2 * TILES], in_=spread[:, 0 : 2 * TILES])
                nc.gpsimd.tensor_tensor(factors[:, 2 * TILES :], factors[:, 0:TILES], factors[:, TILES : 2 * TILES], ALU.mult)
            if i > 1:
                pick(i - 2, 0, NP)
            if i > 0:
                feature(i - 1)
            if i < TILES:
                wobble(i)
            if i % 2 == 0 and i + 2 < TILES:
                woven["w1"] = weave_first(raw1[i // 2 + 1])
                woven["w3"] = weave_first(raw3[i // 2 + 1])
            if i == 0:
                for a in range(2):
                    raw5[a, 0] = load_weight(w5, a, 0, PASS, "raw5", 2)
                for q in range(4):
                    nc.sync.dma_start(
                        out=w4s[32 * q : 32 * q + 4, :, :].bitcast(I32),
                        in_=w4_scales[:, 4 * q : 4 * q + 4, :].rearrange("a r c -> r a c").bitcast(I32),
                    )
                nc.sync.dma_start(out=w4w[:].bitcast(I32), in_=w4_words.rearrange("a p c -> p a c").bitcast(I32))
                nc.sync.dma_start(out=wgo_sb[:], in_=wgo)
            if i + 4 < TILES:
                speeds[i + 4] = load_speed(i + 4)
            if i in (1, 3, 5, 6):
                b, a = divmod((1, 3, 5, 6).index(i), 2)
                for part in range(2):
                    weave_second(a, b, part)
                if b == 0:
                    raw5[a, 1] = load_weight(w5, a, PASS, PASS, "raw5", 2)
            if i == 5:
                woven["x0"] = [turn_back(0, half) for half in range(2)]

        last = TILES - 1
        for half in range(2):
            pick(last, half * HALF, (half + 1) * HALF)
        woven["x1"] = [turn_back(1, half) for half in range(2)]
        for half in range(2):
            quantise_x(0, half, woven["x0"][half])
        codes5 = held.tile([P, 4, PASS], U32, name="last_larger", align_bytes=64)

        def quantise_second(a, b):
            scales5 = held.tile([P, PASS], U8, name="scales_w5_%d%d" % (a, b), align_bytes=64)
            nc.vector.quantize_mx(out=codes5[:, 2 * b + a, :].bitcast(FP8X4), scales=scales5[:], in_=woven[a, b][:])
            q5[a, b] = (codes5[:, 2 * b + a, :], scales5)

        for a in range(2):
            quantise_second(a, 0)

        ys, pages = {}, {}

        def second_products(i, m0, m1):
            b, t = divmod(i, PACK)
            cols, wide, ms = slice(t * P, (t + 1) * P), slice(i * P, (i + 1) * P), slice(m0, m1)
            y1 = psum.tile([P, m1 - m0], F32, name="phase" if i == 0 else "left")
            for a in range(2):
                mx(y1[:], w4w[:, a, wide].bitcast(FP4X4), w4s[:, a, wide], xq[a][0][:, ms].bitcast(FP8X4), xq[a][1][:, ms], a == 0, a == 1)
            y2 = psum.tile([P, m1 - m0], F32, name="right")
            for a in range(2):
                mx(y2[:], q5[a, b][0][:, cols].bitcast(FP8X4), q5[a, b][1][:, cols], xq[a][0][:, ms].bitcast(FP8X4), xq[a][1][:, ms], a == 0, a == 1)
            if i == 0:
                y = held.tile([P, m1 - m0], F32, name="page%d" % (1 + m0 // HALF))
            else:
                y = ring.tile([P, m1 - m0], F32, name="y", bufs=4)
            nc.scalar.copy(out=y[:], in_=y1[:])
            nc.vector.tensor_tensor(y[:], y2[:], y[:], ALU.max)
            ys[i, m0] = y

        def make_page(i):
            pages[i] = held.tile([P, S], F32, name="page%d" % (i % 3))
            col = TILES + i if i == TILES - 1 else 2 * TILES + i
            nc.scalar.activation(pages[i][:], us[i][:], ACT.Copy, scale=factors[:, col : col + 1])

        def put(i, m0, m1):
            nc.vector.tensor_tensor(pages[i][:].indirect(p1[:, m0 // 16 : m1 // 16]), ys[i, m0][:], wgo_sb[:, m0:m1], ALU.mult)

        make_page(0)
        for half in range(2):
            quantise_x(1, half, woven["x1"][half])
            second_products(0, half * HALF, (half + 1) * HALF)
        put(0, 0, HALF)
        for i in range(TILES):
            if i + 1 < TILES:
                second_products(i + 1, 0, NP)
            if i == 0:
                put(0, HALF, NP)
            else:
                make_page(i)
                put(i, 0, NP)
            nc.sync.dma_start(out=out[i * P : (i + 1) * P, :], in_=pages[i][:])
            if i in (1, 2):
                quantise_second(i - 1, 1)
